import numpy as np
import ml_dtypes


def mxq(x, axis, fmt="e4m3"):
    dtype, down = {"e4m3": (ml_dtypes.float8_e4m3fn, 7), "e5m2": (ml_dtypes.float8_e5m2, 14)}[fmt]
    v = np.moveaxis(np.asarray(x, np.float32).astype(ml_dtypes.bfloat16).astype(np.float64), axis, -1)
    blocks = v.reshape(v.shape[:-1] + (-1, 32))
    amax = np.abs(blocks).max(-1, keepdims=True)
    byte = np.maximum(np.where(amax > 0, np.frexp(amax)[1] - 1 + 127, 0) - down, 1)
    scale = np.exp2(byte - 127.0)
    codes = (blocks / scale).astype(np.float32).astype(dtype).astype(np.float64)
    return np.moveaxis((codes * scale).reshape(v.shape), -1, axis)


WIDE = False


def mx_kscale(k):
    if not WIDE:
        return np.ones(k)
    levels = np.array([10, -10, 5, -5, 0])
    if k % 512:
        return np.exp2(np.random.permutation(np.resize(levels, k // 32))).repeat(32)
    a = np.empty((k // 512, 16))
    for p in range(k // 512):
        a[p, :8] = np.random.permutation(np.resize(levels, 8))
        for g in range(8):
            far = levels[np.abs(levels - a[p, g]) >= 10]
            a[p, g + 8] = far[np.random.randint(len(far))]
    return np.exp2(a.ravel()).repeat(32)


def f64(x):
    return np.asarray(x).astype(np.float64)


def striped(idx):
    return np.tile(np.asarray(idx).reshape(-1, 16).T, (8, 1)).astype(np.uint16)


def unstriped(offs):
    return offs[:16].T.reshape(-1).astype(np.int64)


def striped8(idx):
    return np.asarray(idx).reshape(8, -1, 16).transpose(0, 2, 1).reshape(128, -1).astype(np.uint16)


def unstriped8(offs):
    return offs.reshape(8, 16, -1).transpose(0, 2, 1).reshape(8, -1).astype(np.int64)


def pick8(x, idx, run):
    r = np.arange(len(x))
    return x[r[:, None], idx[r % (8 * run) // run]]


E2M1 = np.array([0.0, 0.5, 1.0, 1.5, 2.0, 3.0, 4.0, 6.0, -0.0, -0.5, -1.0, -1.5, -2.0, -3.0, -4.0, -6.0])


def pack_weight(w, fmt):
    k, n = w.shape
    w = f64(np.asarray(w, np.float32).astype(ml_dtypes.bfloat16)).reshape(k // 32, 32, n)
    amax = np.abs(w).max(1)
    if fmt == "e4m3":
        byte = np.frexp(amax)[1] - 1 + 127 - 7
    else:
        mant, ex = np.frexp(amax / 6.0)
        byte = np.where(mant > 0.5, ex, ex - 1) + 127
    byte = np.clip(np.where(amax > 0, byte, 1), 1, 254)
    scaled = (w * np.exp2(127.0 - byte)[:, None, :]).reshape(k, n).astype(np.float32)
    by_word = np.ascontiguousarray(scaled.reshape(k // 512, 128, 4, n).transpose(0, 1, 3, 2))
    if fmt == "e4m3":
        words = by_word.astype(ml_dtypes.float8_e4m3fn).view(np.uint8)
    else:
        c = by_word.astype(ml_dtypes.float4_e2m1fn).view(np.uint8) & 0xF
        words = (c[..., 0::2] | (c[..., 1::2] << 4)).reshape(k // 512, 128, 2 * n)
    return np.ascontiguousarray(words), np.ascontiguousarray(byte.astype(np.uint8).reshape(k // 512, 16, n))


def unpack_weight(words, scales, fmt):
    g, _, n = scales.shape
    words = np.ascontiguousarray(words).reshape(g, 128, n, -1)
    if fmt == "e4m3":
        vals = words.view(ml_dtypes.float8_e4m3fn).astype(np.float64)
    else:
        nib = np.empty((g, 128, n, 4), np.uint8)
        nib[..., 0::2] = words & 0xF
        nib[..., 1::2] = words >> 4
        vals = E2M1[nib]
    vals = vals * np.repeat(np.exp2(scales.astype(np.float64) - 127.0), 8, axis=1)[..., None]
    return vals.transpose(0, 1, 3, 2).reshape(g * 512, n)


K, J, R, T, O, N, E, U = 512, 512, 512, 2048, 256, 256, 128, 256


def setup_inputs():
    n = np.random.standard_normal
    idx = np.random.permutation(T)[:J]
    idx2 = np.stack([np.random.permutation(J)[:O] for _ in range(8)])
    idx3 = np.stack([np.random.permutation(J)[:O] for _ in range(8)])
    idx4 = np.stack([np.random.permutation(O)[:E] for _ in range(8)])
    idx5 = np.stack([np.random.permutation(O)[:E] for _ in range(8)])
    idx6 = np.stack([np.random.permutation(U)[:E] for _ in range(8)])
    idx7 = np.stack([np.random.permutation(U)[:E] for _ in range(8)])
    fk = mx_kscale(K)
    fr = mx_kscale(R)
    xtp = pack_weight(n((K, T)) * fk[:, None], "e2m1")
    wp = pack_weight(n((K, R)) * 1 / np.sqrt(K) / fk[:, None] * fr, "e4m3")
    w2p = pack_weight(n((K, R)) * 1 / np.sqrt(K) / fk[:, None] * fr, "e4m3")
    wbp = pack_weight(n((R, N)) * 1 / np.sqrt(R) / fr[:, None], "e2m1")
    return {
        "xt_words": xtp[0],
        "xt_scales": xtp[1],
        "w_words": wp[0],
        "w_scales": wp[1],
        "w2_words": w2p[0],
        "w2_scales": w2p[1],
        "sa": (np.random.uniform(0.5, 1.6, (R, 1))).astype(np.float32),
        "sb": (np.random.uniform(0.5, 1.6, (R, 1))).astype(np.float32),
        "wb_words": wbp[0],
        "wb_scales": wbp[1],
        "se": (np.random.uniform(0.5, 1.6, (N, 1))).astype(np.float32),
        "sf": (np.random.uniform(0.5, 1.6, (N, 1))).astype(np.float32),
        "offs": striped(idx),
        "offs2": striped8(idx2),
        "offs3": striped8(idx3),
        "offs4": striped8(idx4),
        "offs5": striped8(idx5),
        "offs6": striped8(idx6),
        "offs7": striped8(idx7),
    }


def reference(xt_words, xt_scales, w_words, w_scales, w2_words, w2_scales, sa, sb, wb_words, wb_scales, se, sf, offs, offs2, offs3, offs4, offs5, offs6, offs7):
    idx = unstriped(offs)
    idx2 = unstriped8(offs2)
    idx3 = unstriped8(offs3)
    idx4 = unstriped8(offs4)
    idx5 = unstriped8(offs5)
    idx6 = unstriped8(offs6)
    idx7 = unstriped8(offs7)
    xtu = unpack_weight(xt_words, xt_scales, "e2m1")
    wu = unpack_weight(w_words, w_scales, "e4m3")
    w2u = unpack_weight(w2_words, w2_scales, "e4m3")
    wbu = unpack_weight(wb_words, wb_scales, "e2m1")
    xtidxg = xtu[:, idx]
    a = wu.T @ xtidxg
    b = w2u.T @ xtidxg
    hid = np.maximum(pick8(a, idx2, 64) * f64(sa), pick8(b, idx3, 64) * f64(sb))
    hidq = mxq(hid, 0, "e4m3")
    p = wbu.T @ hidq
    q1 = pick8(p, idx4, 16) * f64(se)
    q2 = pick8(p, idx5, 16) * f64(sf)
    lo = np.minimum(q1, q2)
    hi = np.maximum(q1, q2)
    m0 = np.zeros((N, U))
    m0[np.arange(N)[:, None], idx6[np.arange(N) % 128 // 16]] = lo
    m1 = np.zeros((N, U))
    m1[np.arange(N)[:, None], idx7[np.arange(N) % 128 // 16]] = hi
    y = m0 + m1
    return y

@@ -1,0 +1,199 @@
+from contextlib import ExitStack
+
+import concourse.mybir as mybir
+
+K, J, R, T, O, N, E, U = 512, 512, 512, 2048, 256, 256, 128, 256
+FLOPS = 2 * (2 * K * R * J + R * N * O)
+
+F32 = mybir.dt.float32
+BF16 = mybir.dt.bfloat16
+I32 = mybir.dt.int32
+U32 = mybir.dt.uint32
+U16 = mybir.dt.uint16
+U8 = mybir.dt.uint8
+FP8X4 = mybir.dt.float8_e4m3fn_x4
+FP4X4 = mybir.dt.float4_e2m1fn_x4
+COPY = mybir.ActivationFunctionType.Copy
+ALU = mybir.AluOpType
+
+P = 128
+PACK = 4
+HALF = O // 2
+
+
+def load_scale_rows(queues, plane, scales):
+    for i, queue in enumerate(queues):
+        queue.dma_start(out=plane[i:P:32, :].bitcast(I32), in_=scales[0, i:16:4, :].bitcast(I32))
+
+
+def tile_picked_tokens_plain_twin_groupmeet_one_endexchange_kernel(
+    tc, xt_words, xt_scales, w_words, w_scales, w2_words, w2_scales, sa, sb, wb_words, wb_scales, se, sf,
+    offs, offs2, offs3, offs4, offs5, offs6, offs7, out,
+):
+    nc = tc.nc
+    with ExitStack() as ctx:
+        lists = ctx.enter_context(tc.tile_pool(name="lists", bufs=1))
+        keep = ctx.enter_context(tc.tile_pool(name="keep", bufs=1))
+        psum = ctx.enter_context(tc.psum_pool(name="psum", bufs=1))
+
+        def load_list(src, name):
+            tile = lists.tile(list(src.shape), U16, name=name)
+            nc.sync.dma_start(tile[:], src)
+            return tile
+
+        x_scales = keep.tile([P, T], U8, name="x_scales", align_bytes=64)
+        x_words = keep.tile([P, 2 * T], U8, name="x_words", align_bytes=64)
+        raw_scales = [keep.tile([P, R], U8, name="raw_scales%d" % i, align_bytes=64) for i in range(2)]
+        raw_words = [keep.tile([P, R], U32, name="raw_words%d" % i, align_bytes=64) for i in range(2)]
+        b_scales = keep.tile([P, N], U8, name="b_scales", align_bytes=64)
+        b_words = keep.tile([P, 2 * N], U8, name="b_words", align_bytes=64)
+        pages = [[keep.tile([P, U], F32, name="page%d_%d" % (s, nb)) for s in range(2)] for nb in range(2)]
+
+        nc.vector.memset(x_scales[:, : T // 2].bitcast(I32), 0)
+        nc.gpsimd.memset(x_scales[:, T // 2 :].bitcast(I32), 0)
+        for plane in raw_scales + [b_scales]:
+            nc.vector.memset(plane[:].bitcast(I32), 0)
+        for nb in range(2):
+            for s in range(2):
+                nc.vector.memset(pages[nb][s][:], 0.0)
+
+        tok_list = load_list(offs, "tok_list")
+        load_scale_rows([nc.sync, nc.sync, nc.scalar, nc.scalar], x_scales, xt_scales)
+        nc.sync.dma_start(out=x_words[:].bitcast(I32), in_=xt_words[0].bitcast(I32))
+        nc.sync.dma_start(out=raw_words[0][:].bitcast(I32), in_=w_words[0].rearrange("p n t -> p (n t)").bitcast(I32))
+        load_scale_rows([nc.scalar, nc.scalar, nc.sync, nc.sync], raw_scales[0], w_scales)
+        nc.sync.dma_start(out=raw_words[1][:].bitcast(I32), in_=w2_words[0].rearrange("p n t -> p (n t)").bitcast(I32))
+        slot_lists = [load_list(offs2, "slot_list0")]
+        load_scale_rows([nc.sync] * 4, raw_scales[1], w2_scales)
+        slot_lists.append(load_list(offs3, "slot_list1"))
+        hid_gain = []
+        for i, vec in enumerate((sa, sb)):
+            gain = keep.tile([P, PACK], F32, name="hid_gain%d" % i)
+            nc.gpsimd.dma_start(out=gain[:], in_=vec.rearrange("(p t) o -> p (t o)", t=PACK))
+            hid_gain.append(gain)
+        out_gain = []
+        for i, vec in enumerate((se, sf)):
+            gain = keep.tile([P, 2], F32, name="out_gain%d" % i)
+            with nc.allow_non_contiguous_dma(reason="one value a partition for each block of 128 features"):
+                nc.sync.dma_start(out=gain[:], in_=vec.rearrange("(b p) o -> p (b o)", p=P))
+            out_gain.append(gain)
+        nc.sync.dma_start(out=b_words[:].bitcast(I32), in_=wb_words[0].bitcast(I32))
+        load_scale_rows([nc.sync] * 4, b_scales, wb_scales)
+        place_lists = [load_list(offs4, "place_list0"), load_list(offs5, "place_list1")]
+        page_lists = [load_list(offs6, "page_list0"), load_list(offs7, "page_list1")]
+
+        g_scales = keep.tile([P, J], U8, name="g_scales", align_bytes=64)
+        g_words = keep.tile([P, 2 * J], U8, name="g_words", align_bytes=64)
+        nc.vector.tensor_copy(out=g_scales[:], in_=x_scales[:].indirect(tok_list[:]))
+        nc.vector.tensor_copy(out=g_words[:].bitcast(U16), in_=x_words[:].bitcast(U16).indirect(tok_list[:]))
+
+        dealt_words = [keep.tile([P, R], U32, name="dealt_words%d" % i, align_bytes=64) for i in range(2)]
+        dealt_scales = [keep.tile([P, R], U8, name="dealt_scales%d" % i, align_bytes=64) for i in range(2)]
+        nc.scalar.copy(
+            out=dealt_words[0][:].rearrange("p (t m) -> p m t", t=PACK),
+            in_=raw_words[0][:].rearrange("p (m t) -> p m t", t=PACK),
+        )
+
+        def deal(dst, src, t0, t1):
+            nc.gpsimd.tensor_copy(
+                out=dst[:].rearrange("p (t m) -> p t m", t=PACK)[:, t0:t1, :],
+                in_=src[:].rearrange("p (m t) -> p t m", t=PACK)[:, t0:t1, :],
+            )
+
+        deal(dealt_scales[0], raw_scales[0], 0, 2)
+        deal(dealt_scales[0], raw_scales[0], 2, 4)
+        deal(dealt_words[1], raw_words[1], 0, 4)
+        deal(dealt_scales[1], raw_scales[1], 0, 4)
+
+        order = [(i, t) for i in range(2) for t in range(PACK)]
+        rows = {}
+        used_banks = []
+
+        def next_bank(width):
+            used_banks.append(psum.tile([P, width], F32, name="acc", tag="bank%d" % (len(used_banks) % 8)))
+            return used_banks[-1]
+
+        for i, t in order:
+            cols = slice(t * P, (t + 1) * P)
+            row = keep.tile([P, J], F32, name="rows%d_%d" % (i, t))
+            first = (i, t) == order[0]
+            for j0, j1 in ((0, J // 2), (J // 2, J)) if first else ((0, J),):
+                acc = next_bank(j1 - j0)
+                nc.tensor.matmul_mx(
+                    out=acc[:], lhsT=dealt_words[i][:, cols].bitcast(FP8X4), lhsT_scale=dealt_scales[i][:, cols],
+                    rhs=g_words[:, 2 * j0 : 2 * j1].bitcast(FP4X4), rhs_scale=g_scales[:, j0:j1], start=True, stop=True,
+                )
+                if first and j0 == 0:
+                    nc.scalar.copy(out=row[:, j0:j1], in_=acc[:])
+                else:
+                    nc.vector.tensor_copy(out=row[:, j0:j1], in_=acc[:])
+            rows[(i, t)] = row
+
+        early = [keep.tile([P, 2, O], F32, name="early%d" % i) for i in range(2)]
+        late_a = keep.tile([P, 2, O], F32, name="late_a")
+        late_b = [keep.tile([P, 2, HALF], F32, name="late_b%d" % h) for h in range(2)]
+
+        def fetch(dst, i, t, offsets):
+            nc.scalar.activation(
+                out=dst, in_=rows[(i, t)][:].indirect(offsets), func=COPY, scale=hid_gain[i][:, t : t + 1]
+            )
+
+        for t in range(PACK):
+            fetch((early[0] if t < 2 else late_a)[:, t % 2, :], 0, t, slot_lists[0][:])
+        for t in range(2):
+            fetch(early[1][:, t, :], 1, t, slot_lists[1][:])
+        for h in range(2):
+            for t in (2, 3):
+                fetch(late_b[h][:, t - 2, :], 1, t, slot_lists[1][:, h * 8 : (h + 1) * 8])
+
+        pairs = [keep.tile([P, 2, HALF, 2], BF16, name="pairs%d" % h) for h in range(2)]
+        for h in range(2):
+            pair = [early[i][:, :, h * HALF : (h + 1) * HALF].rearrange("p t o -> p o t") for i in range(2)]
+            nc.vector.tensor_tensor(out=pairs[h][:, 0, :, :], in0=pair[0], in1=pair[1], op=ALU.max)
+        p_rows = [keep.tile([P, O], F32, name="p_rows%d" % nb) for nb in range(2)]
+        for h in range(2):
+            pair = [late_a[:, :, h * HALF : (h + 1) * HALF], late_b[h][:]]
+            pair = [v.rearrange("p t o -> p o t") for v in pair]
+            nc.vector.tensor_tensor(out=pairs[h][:, 1, :, :], in0=pair[0], in1=pair[1], op=ALU.max)
+            hid = keep.tile([P, HALF, PACK], BF16, name="hid%d" % h, align_bytes=64)
+            nc.vector.tensor_copy(
+                out=hid[:].rearrange("p o t -> p (o t)").bitcast(I32).rearrange("p (o u) -> p o u", u=2),
+                in_=pairs[h][:].rearrange("p u o t -> p (u o t)").bitcast(I32).rearrange("p (u o) -> p o u", u=2),
+            )
+            codes = keep.tile([P, HALF], U32, name="hid_codes%d" % h, align_bytes=64)
+            scales = keep.tile([P, HALF], U8, name="hid_scales%d" % h, align_bytes=64)
+            nc.vector.quantize_mx(
+                out=codes[:].bitcast(FP8X4), scales=scales[:], in_=hid[:].rearrange("p o t -> p (o t)")
+            )
+            for nb in range(2):
+                acc = next_bank(HALF)
+                nc.tensor.matmul_mx(
+                    out=acc[:],
+                    lhsT=b_words[:, nb * 2 * P : (nb + 1) * 2 * P].bitcast(FP4X4),
+                    lhsT_scale=b_scales[:, nb * P : (nb + 1) * P],
+                    rhs=codes[:].bitcast(FP8X4), rhs_scale=scales[:], start=True, stop=True,
+                )
+                dst = p_rows[nb][:, h * HALF : (h + 1) * HALF]
+                if (h, nb) == (1, 1):
+                    nc.vector.tensor_copy(out=dst, in_=acc[:])
+                else:
+                    nc.scalar.copy(out=dst, in_=acc[:])
+
+        ends = []
+        for nb in range(2):
+            q = [keep.tile([P, E], F32, name="q%d_%d" % (nb, s)) for s in range(2)]
+            for s in range(2):
+                nc.scalar.activation(
+                    out=q[s][:], in_=p_rows[nb][:].indirect(place_lists[s][:]), func=COPY,
+                    scale=out_gain[s][:, nb : nb + 1],
+                )
+            lo_hi = [keep.tile([P, E], F32, name="lo_hi%d_%d" % (nb, s)) for s in range(2)]
+            for s, op in enumerate((ALU.min, ALU.max)):
+                nc.vector.tensor_tensor(out=lo_hi[s][:], in0=q[0][:], in1=q[1][:], op=op)
+            ends.append(lo_hi)
+        for nb in range(2):
+            for s in range(2):
+                nc.scalar.activation(out=pages[nb][s][:].indirect(page_lists[s][:]), in_=ends[nb][s][:], func=COPY)
+            total = keep.tile([P, U], F32, name="total%d" % nb)
+            nc.vector.tensor_tensor(out=total[:], in0=pages[nb][0][:], in1=pages[nb][1][:], op=ALU.add)
+            nc.sync.dma_start(out=out[nb * P : (nb + 1) * P, :], in_=total[:])

@@ -89,21 +89,21 @@ def tile_picked_tokens_plain_twin_groupmeet_one_endexchange_kernel(
 
         dealt_words = [keep.tile([P, R], U32, name="dealt_words%d" % i, align_bytes=64) for i in range(2)]
         dealt_scales = [keep.tile([P, R], U8, name="dealt_scales%d" % i, align_bytes=64) for i in range(2)]
-        nc.scalar.copy(
-            out=dealt_words[0][:].rearrange("p (t m) -> p m t", t=PACK),
-            in_=raw_words[0][:].rearrange("p (m t) -> p m t", t=PACK),
-        )
+        for i in range(2):
+            nc.scalar.copy(
+                out=dealt_words[i][:].rearrange("p (t m) -> p m t", t=PACK),
+                in_=raw_words[i][:].rearrange("p (m t) -> p m t", t=PACK),
+            )
 
-        def deal(dst, src, t0, t1):
-            nc.gpsimd.tensor_copy(
+        def deal(engine, dst, src, t0, t1):
+            engine.tensor_copy(
                 out=dst[:].rearrange("p (t m) -> p t m", t=PACK)[:, t0:t1, :],
                 in_=src[:].rearrange("p (m t) -> p t m", t=PACK)[:, t0:t1, :],
             )
 
-        deal(dealt_scales[0], raw_scales[0], 0, 2)
-        deal(dealt_scales[0], raw_scales[0], 2, 4)
-        deal(dealt_words[1], raw_words[1], 0, 4)
-        deal(dealt_scales[1], raw_scales[1], 0, 4)
+        deal(nc.vector, dealt_scales[0], raw_scales[0], 0, 2)
+        deal(nc.vector, dealt_scales[0], raw_scales[0], 2, 4)
+        deal(nc.gpsimd, dealt_scales[1], raw_scales[1], 0, 4)
 
         order = [(i, t) for i in range(2) for t in range(PACK)]
         rows = {}

@@ -43,7 +43,8 @@ def tile_picked_tokens_plain_twin_groupmeet_one_endexchange_kernel(
 
         x_scales = keep.tile([P, T], U8, name="x_scales", align_bytes=64)
         x_words = keep.tile([P, 2 * T], U8, name="x_words", align_bytes=64)
-        raw_scales = [keep.tile([P, R], U8, name="raw_scales%d" % i, align_bytes=64) for i in range(2)]
+        w_staged = keep.tile([4, 4, R], U8, name="w_staged")
+        w_planes = [keep.tile([P, R], U8, name="w_plane%d" % i) for i in range(2)]
         raw_words = [keep.tile([P, R], U32, name="raw_words%d" % i, align_bytes=64) for i in range(2)]
         b_scales = keep.tile([P, N], U8, name="b_scales", align_bytes=64)
         b_words = keep.tile([P, 2 * N], U8, name="b_words", align_bytes=64)
@@ -51,20 +52,23 @@ def tile_picked_tokens_plain_twin_groupmeet_one_endexchange_kernel(
 
         nc.vector.memset(x_scales[:, : T // 2].bitcast(I32), 0)
         nc.gpsimd.memset(x_scales[:, T // 2 :].bitcast(I32), 0)
-        for plane in raw_scales + [b_scales]:
+        for plane in w_planes + [b_scales]:
             nc.vector.memset(plane[:].bitcast(I32), 0)
         for nb in range(2):
             for s in range(2):
                 nc.vector.memset(pages[nb][s][:], 0.0)
 
+        def load_words(queue, i, words):
+            queue.dma_start(out=raw_words[i][:].bitcast(I32), in_=words[0].rearrange("p n t -> p (n t)").bitcast(I32))
+
+        nc.sync.dma_start(out=w_staged[:].bitcast(I32), in_=w_scales[0].rearrange("(q i) c -> i q c", i=4).bitcast(I32))
         tok_list = load_list(offs, "tok_list")
-        load_scale_rows([nc.sync, nc.sync, nc.scalar, nc.scalar], x_scales, xt_scales)
         nc.sync.dma_start(out=x_words[:].bitcast(I32), in_=xt_words[0].bitcast(I32))
-        nc.sync.dma_start(out=raw_words[0][:].bitcast(I32), in_=w_words[0].rearrange("p n t -> p (n t)").bitcast(I32))
-        load_scale_rows([nc.scalar, nc.scalar, nc.sync, nc.sync], raw_scales[0], w_scales)
-        nc.sync.dma_start(out=raw_words[1][:].bitcast(I32), in_=w2_words[0].rearrange("p n t -> p (n t)").bitcast(I32))
+        load_words(nc.sync, 0, w_words)
+        load_scale_rows([nc.sync] * 4, x_scales, xt_scales)
+        load_words(nc.sync, 1, w2_words)
         slot_lists = [load_list(offs2, "slot_list0")]
-        load_scale_rows([nc.sync] * 4, raw_scales[1], w2_scales)
+        load_scale_rows([nc.sync] * 4, w_planes[1], w2_scales)
         slot_lists.append(load_list(offs3, "slot_list1"))
         hid_gain = []
         for i, vec in enumerate((sa, sb)):
@@ -77,15 +81,19 @@ def tile_picked_tokens_plain_twin_groupmeet_one_endexchange_kernel(
             with nc.allow_non_contiguous_dma(reason="one value a partition for each block of 128 features"):
                 nc.sync.dma_start(out=gain[:], in_=vec.rearrange("(b p) o -> p (b o)", p=P))
             out_gain.append(gain)
-        nc.sync.dma_start(out=b_words[:].bitcast(I32), in_=wb_words[0].bitcast(I32))
-        load_scale_rows([nc.sync] * 4, b_scales, wb_scales)
         place_lists = [load_list(offs4, "place_list0"), load_list(offs5, "place_list1")]
         page_lists = [load_list(offs6, "page_list0"), load_list(offs7, "page_list1")]
+        nc.sync.dma_start(out=b_words[:].bitcast(I32), in_=wb_words[0].bitcast(I32))
+        load_scale_rows([nc.sync] * 4, b_scales, wb_scales)
 
-        g_scales = keep.tile([P, J], U8, name="g_scales", align_bytes=64)
         g_words = keep.tile([P, 2 * J], U8, name="g_words", align_bytes=64)
-        nc.vector.tensor_copy(out=g_scales[:], in_=x_scales[:].indirect(tok_list[:]))
         nc.vector.tensor_copy(out=g_words[:].bitcast(U16), in_=x_words[:].bitcast(U16).indirect(tok_list[:]))
+        g_scales = keep.tile([P, J], U8, name="g_scales", align_bytes=64)
+        for h in range(2):
+            nc.vector.tensor_copy(
+                out=g_scales[:, h * J // 2 : (h + 1) * J // 2],
+                in_=x_scales[:].indirect(tok_list[:, h * 16 : (h + 1) * 16]),
+            )
 
         dealt_words = [keep.tile([P, R], U32, name="dealt_words%d" % i, align_bytes=64) for i in range(2)]
         dealt_scales = [keep.tile([P, R], U8, name="dealt_scales%d" % i, align_bytes=64) for i in range(2)]
@@ -95,15 +103,13 @@ def tile_picked_tokens_plain_twin_groupmeet_one_endexchange_kernel(
                 in_=raw_words[i][:].rearrange("p (m t) -> p m t", t=PACK),
             )
 
-        def deal(engine, dst, src, t0, t1):
-            engine.tensor_copy(
-                out=dst[:].rearrange("p (t m) -> p t m", t=PACK)[:, t0:t1, :],
-                in_=src[:].rearrange("p (m t) -> p t m", t=PACK)[:, t0:t1, :],
+        for q in range(4):
+            nc.vector.tensor_copy(out=w_planes[0][32 * q : 32 * q + 4, :].bitcast(I32), in_=w_staged[:, q, :].bitcast(I32))
+        for i, plane in enumerate(w_planes):
+            nc.gpsimd.tensor_copy(
+                out=dealt_scales[i][:].rearrange("p (t m) -> p t m", t=PACK),
+                in_=plane[:].rearrange("p (m t) -> p t m", t=PACK),
             )
-
-        deal(nc.vector, dealt_scales[0], raw_scales[0], 0, 2)
-        deal(nc.vector, dealt_scales[0], raw_scales[0], 2, 4)
-        deal(nc.gpsimd, dealt_scales[1], raw_scales[1], 0, 4)
 
         order = [(i, t) for i in range(2) for t in range(PACK)]
         rows = {}
@@ -123,10 +129,7 @@ def tile_picked_tokens_plain_twin_groupmeet_one_endexchange_kernel(
                     out=acc[:], lhsT=dealt_words[i][:, cols].bitcast(FP8X4), lhsT_scale=dealt_scales[i][:, cols],
                     rhs=g_words[:, 2 * j0 : 2 * j1].bitcast(FP4X4), rhs_scale=g_scales[:, j0:j1], start=True, stop=True,
                 )
-                if first and j0 == 0:
-                    nc.scalar.copy(out=row[:, j0:j1], in_=acc[:])
-                else:
-                    nc.vector.tensor_copy(out=row[:, j0:j1], in_=acc[:])
+                nc.vector.tensor_copy(out=row[:, j0:j1], in_=acc[:])
             rows[(i, t)] = row
 
         early = [keep.tile([P, 2, O], F32, name="early%d" % i) for i in range(2)]
@@ -151,6 +154,7 @@ def tile_picked_tokens_plain_twin_groupmeet_one_endexchange_kernel(
             pair = [early[i][:, :, h * HALF : (h + 1) * HALF].rearrange("p t o -> p o t") for i in range(2)]
             nc.vector.tensor_tensor(out=pairs[h][:, 0, :, :], in0=pair[0], in1=pair[1], op=ALU.max)
         p_rows = [keep.tile([P, O], F32, name="p_rows%d" % nb) for nb in range(2)]
+        second_block = next_bank(O)
         for h in range(2):
             pair = [late_a[:, :, h * HALF : (h + 1) * HALF], late_b[h][:]]
             pair = [v.rearrange("p t o -> p o t") for v in pair]
@@ -166,18 +170,16 @@ def tile_picked_tokens_plain_twin_groupmeet_one_endexchange_kernel(
                 out=codes[:].bitcast(FP8X4), scales=scales[:], in_=hid[:].rearrange("p o t -> p (o t)")
             )
             for nb in range(2):
-                acc = next_bank(HALF)
+                acc = next_bank(HALF)[:] if nb == 0 else second_block[:, h * HALF : (h + 1) * HALF]
                 nc.tensor.matmul_mx(
-                    out=acc[:],
+                    out=acc,
                     lhsT=b_words[:, nb * 2 * P : (nb + 1) * 2 * P].bitcast(FP4X4),
                     lhsT_scale=b_scales[:, nb * P : (nb + 1) * P],
                     rhs=codes[:].bitcast(FP8X4), rhs_scale=scales[:], start=True, stop=True,
                 )
-                dst = p_rows[nb][:, h * HALF : (h + 1) * HALF]
-                if (h, nb) == (1, 1):
-                    nc.vector.tensor_copy(out=dst, in_=acc[:])
-                else:
-                    nc.scalar.copy(out=dst, in_=acc[:])
+                if nb == 0:
+                    nc.scalar.copy(out=p_rows[0][:, h * HALF : (h + 1) * HALF], in_=acc)
+        nc.vector.tensor_copy(out=p_rows[1][:], in_=second_block[:])
 
         ends = []
         for nb in range(2):

@@ -50,9 +50,7 @@ def tile_picked_tokens_plain_twin_groupmeet_one_endexchange_kernel(
         b_words = keep.tile([P, 2 * N], U8, name="b_words", align_bytes=64)
         pages = [[keep.tile([P, U], F32, name="page%d_%d" % (s, nb)) for s in range(2)] for nb in range(2)]
 
-        nc.vector.memset(x_scales[:, : T // 2].bitcast(I32), 0)
-        nc.gpsimd.memset(x_scales[:, T // 2 :].bitcast(I32), 0)
-        for plane in w_planes + [b_scales]:
+        for plane in [x_scales] + w_planes + [b_scales]:
             nc.vector.memset(plane[:].bitcast(I32), 0)
         for nb in range(2):
             for s in range(2):
@@ -67,14 +65,12 @@ def tile_picked_tokens_plain_twin_groupmeet_one_endexchange_kernel(
         load_words(nc.sync, 0, w_words)
         load_scale_rows([nc.sync] * 4, x_scales, xt_scales)
         load_words(nc.sync, 1, w2_words)
+        hid_gain = [keep.tile([P, PACK], F32, name="hid_gain%d" % i) for i in range(2)]
         slot_lists = [load_list(offs2, "slot_list0")]
+        nc.sync.dma_start(out=hid_gain[0][:], in_=sa.rearrange("(p t) o -> p (t o)", t=PACK))
         load_scale_rows([nc.sync] * 4, w_planes[1], w2_scales)
         slot_lists.append(load_list(offs3, "slot_list1"))
-        hid_gain = []
-        for i, vec in enumerate((sa, sb)):
-            gain = keep.tile([P, PACK], F32, name="hid_gain%d" % i)
-            nc.gpsimd.dma_start(out=gain[:], in_=vec.rearrange("(p t) o -> p (t o)", t=PACK))
-            hid_gain.append(gain)
+        nc.sync.dma_start(out=hid_gain[1][:], in_=sb.rearrange("(p t) o -> p (t o)", t=PACK))
         out_gain = []
         for i, vec in enumerate((se, sf)):
             gain = keep.tile([P, 2], F32, name="out_gain%d" % i)

from contextlib import ExitStack

import concourse.mybir as mybir

K, J, R, T, O, N, E, U = 512, 512, 512, 2048, 256, 256, 128, 256
FLOPS = 2 * (2 * K * R * J + R * N * O)

F32 = mybir.dt.float32
BF16 = mybir.dt.bfloat16
I32 = mybir.dt.int32
U32 = mybir.dt.uint32
U16 = mybir.dt.uint16
U8 = mybir.dt.uint8
FP8X4 = mybir.dt.float8_e4m3fn_x4
FP4X4 = mybir.dt.float4_e2m1fn_x4
COPY = mybir.ActivationFunctionType.Copy
ALU = mybir.AluOpType

P = 128
PACK = 4
HALF = O // 2


def load_scale_rows(queues, plane, scales):
    for i, queue in enumerate(queues):
        queue.dma_start(out=plane[i:P:32, :].bitcast(I32), in_=scales[0, i:16:4, :].bitcast(I32))


def tile_picked_tokens_plain_twin_groupmeet_one_endexchange_kernel(
    tc, xt_words, xt_scales, w_words, w_scales, w2_words, w2_scales, sa, sb, wb_words, wb_scales, se, sf,
    offs, offs2, offs3, offs4, offs5, offs6, offs7, out,
):
    nc = tc.nc
    with ExitStack() as ctx:
        lists = ctx.enter_context(tc.tile_pool(name="lists", bufs=1))
        keep = ctx.enter_context(tc.tile_pool(name="keep", bufs=1))
        psum = ctx.enter_context(tc.psum_pool(name="psum", bufs=1))

        def load_list(src, name):
            tile = lists.tile(list(src.shape), U16, name=name)
            nc.sync.dma_start(tile[:], src)
            return tile

        x_scales = keep.tile([P, T], U8, name="x_scales", align_bytes=64)
        x_words = keep.tile([P, 2 * T], U8, name="x_words", align_bytes=64)
        w_staged = keep.tile([4, 4, R], U8, name="w_staged")
        w_planes = [keep.tile([P, R], U8, name="w_plane%d" % i) for i in range(2)]
        raw_words = [keep.tile([P, R], U32, name="raw_words%d" % i, align_bytes=64) for i in range(2)]
        b_scales = keep.tile([P, N], U8, name="b_scales", align_bytes=64)
        b_words = keep.tile([P, 2 * N], U8, name="b_words", align_bytes=64)
        pages = [[keep.tile([P, U], F32, name="page%d_%d" % (s, nb)) for s in range(2)] for nb in range(2)]

        for plane in [x_scales] + w_planes + [b_scales]:
            nc.vector.memset(plane[:].bitcast(I32), 0)
        for nb in range(2):
            for s in range(2):
                nc.vector.memset(pages[nb][s][:], 0.0)

        def load_words(queue, i, words):
            queue.dma_start(out=raw_words[i][:].bitcast(I32), in_=words[0].rearrange("p n t -> p (n t)").bitcast(I32))

        nc.sync.dma_start(out=w_staged[:].bitcast(I32), in_=w_scales[0].rearrange("(q i) c -> i q c", i=4).bitcast(I32))
        tok_list = load_list(offs, "tok_list")
        nc.sync.dma_start(out=x_words[:].bitcast(I32), in_=xt_words[0].bitcast(I32))
        load_words(nc.sync, 0, w_words)
        load_scale_rows([nc.sync] * 4, x_scales, xt_scales)
        load_words(nc.sync, 1, w2_words)
        hid_gain = [keep.tile([P, PACK], F32, name="hid_gain%d" % i) for i in range(2)]
        slot_lists = [load_list(offs2, "slot_list0")]
        nc.sync.dma_start(out=hid_gain[0][:], in_=sa.rearrange("(p t) o -> p (t o)", t=PACK))
        load_scale_rows([nc.sync] * 4, w_planes[1], w2_scales)
        slot_lists.append(load_list(offs3, "slot_list1"))
        nc.sync.dma_start(out=hid_gain[1][:], in_=sb.rearrange("(p t) o -> p (t o)", t=PACK))
        out_gain = []
        for i, vec in enumerate((se, sf)):
            gain = keep.tile([P, 2], F32, name="out_gain%d" % i)
            with nc.allow_non_contiguous_dma(reason="one value a partition for each block of 128 features"):
                nc.sync.dma_start(out=gain[:], in_=vec.rearrange("(b p) o -> p (b o)", p=P))
            out_gain.append(gain)
        place_lists = [load_list(offs4, "place_list0"), load_list(offs5, "place_list1")]
        page_lists = [load_list(offs6, "page_list0"), load_list(offs7, "page_list1")]
        nc.sync.dma_start(out=b_words[:].bitcast(I32), in_=wb_words[0].bitcast(I32))
        load_scale_rows([nc.sync] * 4, b_scales, wb_scales)

        g_words = keep.tile([P, 2 * J], U8, name="g_words", align_bytes=64)
        nc.vector.tensor_copy(out=g_words[:].bitcast(U16), in_=x_words[:].bitcast(U16).indirect(tok_list[:]))
        g_scales = keep.tile([P, J], U8, name="g_scales", align_bytes=64)
        for h in range(2):
            nc.vector.tensor_copy(
                out=g_scales[:, h * J // 2 : (h + 1) * J // 2],
                in_=x_scales[:].indirect(tok_list[:, h * 16 : (h + 1) * 16]),
            )

        dealt_words = [keep.tile([P, R], U32, name="dealt_words%d" % i, align_bytes=64) for i in range(2)]
        dealt_scales = [keep.tile([P, R], U8, name="dealt_scales%d" % i, align_bytes=64) for i in range(2)]
        for i in range(2):
            nc.scalar.copy(
                out=dealt_words[i][:].rearrange("p (t m) -> p m t", t=PACK),
                in_=raw_words[i][:].rearrange("p (m t) -> p m t", t=PACK),
            )

        for q in range(4):
            nc.vector.tensor_copy(out=w_planes[0][32 * q : 32 * q + 4, :].bitcast(I32), in_=w_staged[:, q, :].bitcast(I32))
        for i, plane in enumerate(w_planes):
            nc.gpsimd.tensor_copy(
                out=dealt_scales[i][:].rearrange("p (t m) -> p t m", t=PACK),
                in_=plane[:].rearrange("p (m t) -> p t m", t=PACK),
            )

        order = [(i, t) for i in range(2) for t in range(PACK)]
        rows = {}
        used_banks = []

        def next_bank(width):
            used_banks.append(psum.tile([P, width], F32, name="acc", tag="bank%d" % (len(used_banks) % 8)))
            return used_banks[-1]

        for i, t in order:
            cols = slice(t * P, (t + 1) * P)
            row = keep.tile([P, J], F32, name="rows%d_%d" % (i, t))
            first = (i, t) == order[0]
            for j0, j1 in ((0, J // 2), (J // 2, J)) if first else ((0, J),):
                acc = next_bank(j1 - j0)
                nc.tensor.matmul_mx(
                    out=acc[:], lhsT=dealt_words[i][:, cols].bitcast(FP8X4), lhsT_scale=dealt_scales[i][:, cols],
                    rhs=g_words[:, 2 * j0 : 2 * j1].bitcast(FP4X4), rhs_scale=g_scales[:, j0:j1], start=True, stop=True,
                )
                nc.vector.tensor_copy(out=row[:, j0:j1], in_=acc[:])
            rows[(i, t)] = row

        early = [keep.tile([P, 2, O], F32, name="early%d" % i) for i in range(2)]
        late_a = keep.tile([P, 2, O], F32, name="late_a")
        late_b = [keep.tile([P, 2, HALF], F32, name="late_b%d" % h) for h in range(2)]

        def fetch(dst, i, t, offsets):
            nc.scalar.activation(
                out=dst, in_=rows[(i, t)][:].indirect(offsets), func=COPY, scale=hid_gain[i][:, t : t + 1]
            )

        for t in range(PACK):
            fetch((early[0] if t < 2 else late_a)[:, t % 2, :], 0, t, slot_lists[0][:])
        for t in range(2):
            fetch(early[1][:, t, :], 1, t, slot_lists[1][:])
        for h in range(2):
            for t in (2, 3):
                fetch(late_b[h][:, t - 2, :], 1, t, slot_lists[1][:, h * 8 : (h + 1) * 8])

        pairs = [keep.tile([P, 2, HALF, 2], BF16, name="pairs%d" % h) for h in range(2)]
        for h in range(2):
            pair = [early[i][:, :, h * HALF : (h + 1) * HALF].rearrange("p t o -> p o t") for i in range(2)]
            nc.vector.tensor_tensor(out=pairs[h][:, 0, :, :], in0=pair[0], in1=pair[1], op=ALU.max)
        p_rows = [keep.tile([P, O], F32, name="p_rows%d" % nb) for nb in range(2)]
        second_block = next_bank(O)
        for h in range(2):
            pair = [late_a[:, :, h * HALF : (h + 1) * HALF], late_b[h][:]]
            pair = [v.rearrange("p t o -> p o t") for v in pair]
            nc.vector.tensor_tensor(out=pairs[h][:, 1, :, :], in0=pair[0], in1=pair[1], op=ALU.max)
            hid = keep.tile([P, HALF, PACK], BF16, name="hid%d" % h, align_bytes=64)
            nc.vector.tensor_copy(
                out=hid[:].rearrange("p o t -> p (o t)").bitcast(I32).rearrange("p (o u) -> p o u", u=2),
                in_=pairs[h][:].rearrange("p u o t -> p (u o t)").bitcast(I32).rearrange("p (u o) -> p o u", u=2),
            )
            codes = keep.tile([P, HALF], U32, name="hid_codes%d" % h, align_bytes=64)
            scales = keep.tile([P, HALF], U8, name="hid_scales%d" % h, align_bytes=64)
            nc.vector.quantize_mx(
                out=codes[:].bitcast(FP8X4), scales=scales[:], in_=hid[:].rearrange("p o t -> p (o t)")
            )
            for nb in range(2):
                acc = next_bank(HALF)[:] if nb == 0 else second_block[:, h * HALF : (h + 1) * HALF]
                nc.tensor.matmul_mx(
                    out=acc,
                    lhsT=b_words[:, nb * 2 * P : (nb + 1) * 2 * P].bitcast(FP4X4),
                    lhsT_scale=b_scales[:, nb * P : (nb + 1) * P],
                    rhs=codes[:].bitcast(FP8X4), rhs_scale=scales[:], start=True, stop=True,
                )
                if nb == 0:
                    nc.scalar.copy(out=p_rows[0][:, h * HALF : (h + 1) * HALF], in_=acc)
        nc.vector.tensor_copy(out=p_rows[1][:], in_=second_block[:])

        ends = []
        for nb in range(2):
            q = [keep.tile([P, E], F32, name="q%d_%d" % (nb, s)) for s in range(2)]
            for s in range(2):
                nc.scalar.activation(
                    out=q[s][:], in_=p_rows[nb][:].indirect(place_lists[s][:]), func=COPY,
                    scale=out_gain[s][:, nb : nb + 1],
                )
            lo_hi = [keep.tile([P, E], F32, name="lo_hi%d_%d" % (nb, s)) for s in range(2)]
            for s, op in enumerate((ALU.min, ALU.max)):
                nc.vector.tensor_tensor(out=lo_hi[s][:], in0=q[0][:], in1=q[1][:], op=op)
            ends.append(lo_hi)
        for nb in range(2):
            for s in range(2):
                nc.scalar.activation(out=pages[nb][s][:].indirect(page_lists[s][:]), in_=ends[nb][s][:], func=COPY)
            total = keep.tile([P, U], F32, name="total%d" % nb)
            nc.vector.tensor_tensor(out=total[:], in0=pages[nb][0][:], in1=pages[nb][1][:], op=ALU.add)
            nc.sync.dma_start(out=out[nb * P : (nb + 1) * P, :], in_=total[:])
